import numpy as np, ml_dtypes
CORES = [16,17,18,19,150,151]
N = 6
KT, C = 4, 128
def setup_inputs(rng):
    return {"x": rng.standard_normal((N, 128, KT * C), dtype=np.float32).astype(ml_dtypes.bfloat16)}
def setup_inputs_big(rng):
    d = setup_inputs(rng)
    for k in ("x",): d[k] = (d[k].astype(np.float32) * 1024.0).astype(d[k].dtype)
    return d
def setup_inputs_small(rng):
    d = setup_inputs(rng)
    for k in ("x",): d[k] = (d[k].astype(np.float32) * (1 / 1024.0)).astype(d[k].dtype)
    return d
def setup_inputs_apart(rng):
    d = setup_inputs(rng)
    f = (10.0 ** rng.permutation(np.linspace(-1.5, 1.5, N))).astype(np.float32).reshape(N, 1, 1)
    for k in ("x",): d[k] = (d[k].astype(np.float32) * f).astype(d[k].dtype)
    return d
def reference(x):
    X = x.astype(np.float64)
    y = np.full((N, C, N * C), np.nan)
    for r in range(N):
        for i in range(N):
            s = i
            if s != r: y[r][:, C * i:C * i + C] = sum(X[r][:, C * t:C * t + C].T @ X[s][:, C * t:C * t + C] for t in range(KT))
    return {"y": y.astype(ml_dtypes.bfloat16 if x.dtype != np.float64 else np.float64)}

@@ -1,0 +1,164 @@
+from concourse.bass import DstId, RemoteDMATransfer
+
+N, KT, C = 6, 4, 128
+W = KT * C
+MAXW = 2
+
+CFG = {
+    "wide": {"cr": 512, "waves": 1, "relay_e": "off", "direct_e": "off", "near_e": "rest", "fwd_e": "all",
+             "order": ("relay0", "relay1", "direct", "near")},
+    "narrow": {"cr": 512, "waves": 1, "relay_e": "off", "direct_e": "off", "near_e": "rest", "fwd_e": "all",
+               "order": ("relay0", "relay1", "direct", "near")},
+}
+
+SCRATCH = {
+    "xs": ("sbuf", [128, N * W], "bfloat16"),
+    "yb": ("sbuf", [128, N * C], "bfloat16"),
+}
+for _s in range(N):
+    SCRATCH["ps%d" % _s] = ("psum", [128, 512], "float32")
+
+SEMAPHORES = ["ld", "sent", "sa", "sb"] + ["c%d" % _k for _k in range(4)]
+for _s in range(N):
+    SEMAPHORES += ["n%d" % _s, "d%d" % _s, "m%d" % _s]
+    SEMAPHORES += ["r%d_%d" % (_s, _w) for _w in range(MAXW)] + ["f%d_%d" % (_s, _w) for _w in range(MAXW)]
+
+
+def _engines(mask):
+    return [e for e in range(mask.bit_length()) if (mask >> e) & 1]
+
+
+def _plan(cores, topo):
+    def where(c):
+        return (topo.host(c), topo.chip(c))
+
+    rank = {c: i for i, c in enumerate(cores)}
+    calls = {c: [] for c in cores}
+    units = {c: [] for c in cores}
+    passon = {c: {} for c in cores}
+    sets, cfgs, peers_of = {}, {}, {}
+    for c in cores:
+        home = [d for d in cores if where(d) == where(c)]
+        far = [d for d in cores if where(d) != where(c)]
+        i = home.index(c)
+        peers = home[i + 1:] + home[:i]
+        off = _engines(topo.mask(c, far[0]))
+        every = _engines(topo.mask(c, peers[0]))
+        es = {"off": off, "all": every, "rest": [e for e in every if e not in off],
+              "off_alt": off[::2], "off_lo": off[:len(off) // 2], "off_hi": off[len(off) // 2:]}
+        cfg = CFG["wide" if len(home) >= len(far) else "narrow"]
+        sets[c], cfgs[c], peers_of[c] = es, cfg, peers
+        q = rank[c]
+        if len(far) <= len(home):
+            relays = [far[i * len(far) // len(home)]]
+        else:
+            k = len(far) // len(home)
+            relays = far[i * k:(i + 1) * k]
+        mine, base, cr, nw = {}, q * W, cfg["cr"], cfg["waves"]
+        for w in range(nw if cr else 0):
+            cw = cr // nw
+            pw = cw // len(relays)
+            e = es[cfg["relay_e"]]
+            share = len(e) // len(relays)
+            sem, trs = "r%d_%d" % (q, w), []
+            for j, d in enumerate(relays):
+                g0 = base + w * cw + j * pw
+                trs.append((g0, g0 + pw, [d], e[j * share:(j + 1) * share], sem))
+                units[d].append((1 + 0.1 * w, sem, share, [(g0, g0 + pw)]))
+                passon[d].setdefault(w, []).append((sem, share, g0, g0 + pw))
+            mine["relay%d" % w] = ([], trs)
+        if cr < W:
+            e = es[cfg["direct_e"]]
+            mine["direct"] = ([], [(base + cr, base + W, far, e, "d%d" % q)])
+            for d in far:
+                units[d].append((2, "d%d" % q, len(e), [(base + cr, base + W)]))
+        e = es[cfg["near_e"]]
+        mine["near"] = ([], [(base, base + W, peers, e, "n%d" % q)])
+        for d in peers:
+            units[d].append((0, "n%d" % q, len(e), [(base, base + W)]))
+        calls[c] = [mine[k] for k in cfg["order"] if k in mine]
+    for c in cores:
+        for w in sorted(passon[c]):
+            got = sorted(passon[c][w], key=lambda p: p[2])
+            runs = []
+            for _sem, _n, g0, g1 in got:
+                if runs and runs[-1][1] == g0:
+                    runs[-1][1] = g1
+                else:
+                    runs.append([g0, g1])
+            e = sets[c][cfgs[c]["fwd_e"]]
+            share = len(e) // len(runs)
+            sem = "f%d_%d" % (rank[c], w)
+            trs = [(g0, g1, peers_of[c], e[j * share:(j + 1) * share], sem) for j, (g0, g1) in enumerate(runs)]
+            calls[c].append(([(p[0], p[1]) for p in got], trs))
+            for d in peers_of[c]:
+                units[d].append((3 + 0.1 * w, sem, share * len(runs), [(g0, g1) for g0, g1 in runs]))
+    return calls, units
+
+
+def rank_program(g, core, T, topo):
+    r = T.rank_of(core)
+    if r is None:
+        return
+    calls, units = _plan(list(T.cores), topo)
+    X, sem = T.xs, T.sem
+
+    g.sync.dma_start(X[:, r * W:(r + 1) * W], T.x[:, :]).then_inc(sem.ld, 16)
+
+    g.wait_ge(sem.ld, 16)
+    left = 0
+    for waits, transfers in calls[core]:
+        for s, n in waits:
+            g.wait_ge(sem[s], n)
+        tl = []
+        for g0, g1, dsts, engs, s in transfers:
+            ids = []
+            for d in dsts:
+                rid, pid = topo.addr(d, core)
+                ids.append(DstId(rid=rid, pnc=pid))
+            mask = 0
+            for e in engs:
+                mask |= 1 << e
+            tl.append(RemoteDMATransfer(dst_ids=ids, dma_engine_mask=mask, remote_sem=sem[s],
+                                        srcs=[X[:, g0:g1]], dsts=[X[:, g0:g1] for _d in dsts]))
+            left += len(engs)
+        g.remote_dma_fused(tl, local_sem=sem.sent)
+    g.wait_ge(sem.sent, left)
+
+    g.tensor.wait_ge(sem.ld, 16)
+    have = {s: 0 for s in range(N)}
+    ended = []
+    for when, s_name, n, ranges in sorted(units[core], key=lambda u: (u[0], u[1])):
+        g.tensor.wait_ge(sem[s_name], n)
+        for g0, g1 in ranges:
+            for col in range(g0, g1, C):
+                s, t = col // W, (col % W) // C
+                mm = g.tensor.matmul(T["ps%d" % s][:, 0:C], X[:, r * W + t * C:r * W + (t + 1) * C], X[:, col:col + C],
+                                     start=(have[s] == 0), stop=(have[s] == KT - 1))
+                have[s] += 1
+                if have[s] == KT:
+                    mm.then_inc(sem["m%d" % s], 1)
+                    ended.append((s, int(when)))
+
+    for s, stage in ended:
+        g.vector.wait_ge(sem["m%d" % s], 1)
+        g.vector.tensor_copy(T.yb[:, s * C:(s + 1) * C], T["ps%d" % s][:, 0:C]).then_inc(sem["c%d" % stage], 1)
+
+    stages = sorted({stage for _s2, stage in ended})
+    count = {"sa": 0, "sb": 0}
+    for stage in stages:
+        q, qs = (g.sync, "sa") if stage == stages[-1] else (g.scalar, "sb")
+        blocks = sorted(s for s, st in ended if st == stage)
+        q.wait_ge(sem["c%d" % stage], len(blocks))
+        b0 = prev = blocks[0]
+        for b in blocks[1:] + [None]:
+            if b is not None and b == prev + 1:
+                prev = b
+                continue
+            q.dma_start(T.y[:, b0 * C:(prev + 1) * C], T.yb[:, b0 * C:(prev + 1) * C]).then_inc(sem[qs], 16)
+            count[qs] += 16
+            b0 = prev = b
+    if count["sa"]:
+        g.sync.wait_ge(sem.sa, count["sa"])
+    if count["sb"]:
+        g.scalar.wait_ge(sem.sb, count["sb"])

@@ -2,13 +2,11 @@ from concourse.bass import DstId, RemoteDMATransfer
 
 N, KT, C = 6, 4, 128
 W = KT * C
-MAXW = 2
+MAXW = 4
 
 CFG = {
-    "wide": {"cr": 512, "waves": 1, "relay_e": "off", "direct_e": "off", "near_e": "rest", "fwd_e": "all",
-             "order": ("relay0", "relay1", "direct", "near")},
-    "narrow": {"cr": 512, "waves": 1, "relay_e": "off", "direct_e": "off", "near_e": "rest", "fwd_e": "all",
-               "order": ("relay0", "relay1", "direct", "near")},
+    "wide": {"waves": (256, 256), "cut": 256, "relay_e": "off", "near_e": "rest", "fwd_e": "all"},
+    "narrow": {"waves": (512,), "cut": 512, "relay_e": "off", "near_e": "rest", "fwd_e": "all"},
 }
 
 SCRATCH = {
@@ -18,9 +16,9 @@ SCRATCH = {
 for _s in range(N):
     SCRATCH["ps%d" % _s] = ("psum", [128, 512], "float32")
 
-SEMAPHORES = ["ld", "sent", "sa", "sb"] + ["c%d" % _k for _k in range(4)]
+SEMAPHORES = ["ld", "ld2", "sent", "sa", "sb"] + ["c%d" % _k for _k in range(4)]
 for _s in range(N):
-    SEMAPHORES += ["n%d" % _s, "d%d" % _s, "m%d" % _s]
+    SEMAPHORES += ["n%d" % _s, "m%d" % _s]
     SEMAPHORES += ["r%d_%d" % (_s, _w) for _w in range(MAXW)] + ["f%d_%d" % (_s, _w) for _w in range(MAXW)]
 
 
@@ -44,39 +42,33 @@ def _plan(cores, topo):
         peers = home[i + 1:] + home[:i]
         off = _engines(topo.mask(c, far[0]))
         every = _engines(topo.mask(c, peers[0]))
-        es = {"off": off, "all": every, "rest": [e for e in every if e not in off],
-              "off_alt": off[::2], "off_lo": off[:len(off) // 2], "off_hi": off[len(off) // 2:]}
+        es = {"off": off, "all": every, "rest": [e for e in every if e not in off]}
         cfg = CFG["wide" if len(home) >= len(far) else "narrow"]
         sets[c], cfgs[c], peers_of[c] = es, cfg, peers
-        q = rank[c]
+        q, base = rank[c], rank[c] * W
+        whole = [("ld", 16)] + ([("ld2", 16)] if cfg["cut"] < W else [])
         if len(far) <= len(home):
             relays = [far[i * len(far) // len(home)]]
         else:
             k = len(far) // len(home)
             relays = far[i * k:(i + 1) * k]
-        mine, base, cr, nw = {}, q * W, cfg["cr"], cfg["waves"]
-        for w in range(nw if cr else 0):
-            cw = cr // nw
+        at = 0
+        for w, cw in enumerate(cfg["waves"]):
             pw = cw // len(relays)
             e = es[cfg["relay_e"]]
             share = len(e) // len(relays)
             sem, trs = "r%d_%d" % (q, w), []
             for j, d in enumerate(relays):
-                g0 = base + w * cw + j * pw
+                g0 = base + at + j * pw
                 trs.append((g0, g0 + pw, [d], e[j * share:(j + 1) * share], sem))
                 units[d].append((1 + 0.1 * w, sem, share, [(g0, g0 + pw)]))
                 passon[d].setdefault(w, []).append((sem, share, g0, g0 + pw))
-            mine["relay%d" % w] = ([], trs)
-        if cr < W:
-            e = es[cfg["direct_e"]]
-            mine["direct"] = ([], [(base + cr, base + W, far, e, "d%d" % q)])
-            for d in far:
-                units[d].append((2, "d%d" % q, len(e), [(base + cr, base + W)]))
+            at += cw
+            calls[c].append((whole[:1] if at <= cfg["cut"] else whole, trs))
         e = es[cfg["near_e"]]
-        mine["near"] = ([], [(base, base + W, peers, e, "n%d" % q)])
+        calls[c].append((whole, [(base, base + W, peers, e, "n%d" % q)]))
         for d in peers:
             units[d].append((0, "n%d" % q, len(e), [(base, base + W)]))
-        calls[c] = [mine[k] for k in cfg["order"] if k in mine]
     for c in cores:
         for w in sorted(passon[c]):
             got = sorted(passon[c][w], key=lambda p: p[2])
@@ -92,20 +84,21 @@ def _plan(cores, topo):
             trs = [(g0, g1, peers_of[c], e[j * share:(j + 1) * share], sem) for j, (g0, g1) in enumerate(runs)]
             calls[c].append(([(p[0], p[1]) for p in got], trs))
             for d in peers_of[c]:
-                units[d].append((3 + 0.1 * w, sem, share * len(runs), [(g0, g1) for g0, g1 in runs]))
-    return calls, units
+                units[d].append((1.05 + 0.1 * w if len(passon[c]) > 1 else 3, sem, share * len(runs), [(g0, g1) for g0, g1 in runs]))
+    return calls, units, cfgs
 
 
 def rank_program(g, core, T, topo):
     r = T.rank_of(core)
     if r is None:
         return
-    calls, units = _plan(list(T.cores), topo)
-    X, sem = T.xs, T.sem
+    calls, units, cfgs = _plan(list(T.cores), topo)
+    X, sem, cut = T.xs, T.sem, cfgs[core]["cut"]
 
-    g.sync.dma_start(X[:, r * W:(r + 1) * W], T.x[:, :]).then_inc(sem.ld, 16)
+    g.sync.dma_start(X[:, r * W:r * W + cut], T.x[:, 0:cut]).then_inc(sem.ld, 16)
+    if cut < W:
+        g.scalar.dma_start(X[:, r * W + cut:(r + 1) * W], T.x[:, cut:W]).then_inc(sem.ld2, 16)
 
-    g.wait_ge(sem.ld, 16)
     left = 0
     for waits, transfers in calls[core]:
         for s, n in waits:
@@ -126,9 +119,12 @@ def rank_program(g, core, T, topo):
     g.wait_ge(sem.sent, left)
 
     g.tensor.wait_ge(sem.ld, 16)
+    if cut < W:
+        g.tensor.wait_ge(sem.ld2, 16)
     have = {s: 0 for s in range(N)}
     ended = []
-    for when, s_name, n, ranges in sorted(units[core], key=lambda u: (u[0], u[1])):
+    todo = sorted(units[core], key=lambda u: (u[0], u[1]))
+    for k, (when, s_name, n, ranges) in enumerate(todo):
         g.tensor.wait_ge(sem[s_name], n)
         for g0, g1 in ranges:
             for col in range(g0, g1, C):
@@ -138,7 +134,7 @@ def rank_program(g, core, T, topo):
                 have[s] += 1
                 if have[s] == KT:
                     mm.then_inc(sem["m%d" % s], 1)
-                    ended.append((s, int(when)))
+                    ended.append((s, 0 if when < 1 else (3 if k == len(todo) - 1 or when >= 3 else 1)))
 
     for s, stage in ended:
         g.vector.wait_ge(sem["m%d" % s], 1)

@@ -3,10 +3,11 @@ from concourse.bass import DstId, RemoteDMATransfer
 N, KT, C = 6, 4, 128
 W = KT * C
 MAXW = 4
+SIM_CORES = 256
 
 CFG = {
-    "wide": {"waves": (256, 256), "cut": 256, "relay_e": "off", "near_e": "rest", "fwd_e": "all"},
-    "narrow": {"waves": (512,), "cut": 512, "relay_e": "off", "near_e": "rest", "fwd_e": "all"},
+    "wide": {"waves": (256, 256), "hand": (3,), "cut": 256, "relay_e": "off", "near_e": "rest", "fwd_e": "all", "hand_e": "rest"},
+    "narrow": {"waves": (512,), "hand": (), "cut": 512, "relay_e": "off", "near_e": "rest", "fwd_e": "all", "hand_e": "rest"},
 }
 
 SCRATCH = {
@@ -16,9 +17,9 @@ SCRATCH = {
 for _s in range(N):
     SCRATCH["ps%d" % _s] = ("psum", [128, 512], "float32")
 
-SEMAPHORES = ["ld", "ld2", "sent", "sa", "sb"] + ["c%d" % _k for _k in range(4)]
+SEMAPHORES = ["ld", "ld2", "sent", "sa", "sb", "h"] + ["c%d" % _k for _k in range(4)]
 for _s in range(N):
-    SEMAPHORES += ["n%d" % _s, "m%d" % _s]
+    SEMAPHORES += ["n%d" % _s, "m%d" % _s, "v%d" % _s]
     SEMAPHORES += ["r%d_%d" % (_s, _w) for _w in range(MAXW)] + ["f%d_%d" % (_s, _w) for _w in range(MAXW)]
 
 
@@ -54,6 +55,16 @@ def _plan(cores, topo):
             relays = far[i * k:(i + 1) * k]
         at = 0
         for w, cw in enumerate(cfg["waves"]):
+            if i in cfg["hand"] and w == len(cfg["waves"]) - 1:
+                k = cfg["hand"].index(i)
+                hc = [d for d in range(SIM_CORES) if where(d) == where(c) and topo.die(d) != topo.die(c) and d not in rank][k]
+                e, eh = es[cfg["hand_e"]], _engines(topo.mask(hc, far[0]))
+                g0, g1 = base + at, base + at + cw
+                calls[c].append((whole, [(g0, g1, [hc], e, "h")]))
+                calls[hc] = [([("h", len(e))], [(g0, g1, far[k % len(far):] + far[:k % len(far)], eh, "v%d" % q)])]
+                for d in far:
+                    units[d].append((1.02 + 0.1 * w, "v%d" % q, len(eh), [(g0, g1)]))
+                continue
             pw = cw // len(relays)
             e = es[cfg["relay_e"]]
             share = len(e) // len(relays)
@@ -88,19 +99,9 @@ def _plan(cores, topo):
     return calls, units, cfgs
 
 
-def rank_program(g, core, T, topo):
-    r = T.rank_of(core)
-    if r is None:
-        return
-    calls, units, cfgs = _plan(list(T.cores), topo)
-    X, sem, cut = T.xs, T.sem, cfgs[core]["cut"]
-
-    g.sync.dma_start(X[:, r * W:r * W + cut], T.x[:, 0:cut]).then_inc(sem.ld, 16)
-    if cut < W:
-        g.scalar.dma_start(X[:, r * W + cut:(r + 1) * W], T.x[:, cut:W]).then_inc(sem.ld2, 16)
-
-    left = 0
-    for waits, transfers in calls[core]:
+def _remote(g, core, T, topo, mine):
+    X, sem, left = T.xs, T.sem, 0
+    for waits, transfers in mine:
         for s, n in waits:
             g.wait_ge(sem[s], n)
         tl = []
@@ -117,6 +118,22 @@ def rank_program(g, core, T, topo):
             left += len(engs)
         g.remote_dma_fused(tl, local_sem=sem.sent)
     g.wait_ge(sem.sent, left)
+
+
+def rank_program(g, core, T, topo):
+    r = T.rank_of(core)
+    calls, units, cfgs = _plan(list(T.cores), topo)
+    if r is None:
+        if core in calls:
+            _remote(g, core, T, topo, calls[core])
+        return
+    X, sem, cut = T.xs, T.sem, cfgs[core]["cut"]
+
+    g.sync.dma_start(X[:, r * W:r * W + cut], T.x[:, 0:cut]).then_inc(sem.ld, 16)
+    if cut < W:
+        g.scalar.dma_start(X[:, r * W + cut:(r + 1) * W], T.x[:, cut:W]).then_inc(sem.ld2, 16)
+
+    _remote(g, core, T, topo, calls[core])
 
     g.tensor.wait_ge(sem.ld, 16)
     if cut < W:

from concourse.bass import DstId, RemoteDMATransfer

N, KT, C = 6, 4, 128
W = KT * C
MAXW = 4
SIM_CORES = 256

CFG = {
    "wide": {"waves": (256, 256), "hand": (3,), "cut": 256, "relay_e": "off", "near_e": "rest", "fwd_e": "all", "hand_e": "rest"},
    "narrow": {"waves": (512,), "hand": (), "cut": 512, "relay_e": "off", "near_e": "rest", "fwd_e": "all", "hand_e": "rest"},
}

SCRATCH = {
    "xs": ("sbuf", [128, N * W], "bfloat16"),
    "yb": ("sbuf", [128, N * C], "bfloat16"),
}
for _s in range(N):
    SCRATCH["ps%d" % _s] = ("psum", [128, 512], "float32")

SEMAPHORES = ["ld", "ld2", "sent", "sa", "sb", "h"] + ["c%d" % _k for _k in range(4)]
for _s in range(N):
    SEMAPHORES += ["n%d" % _s, "m%d" % _s, "v%d" % _s]
    SEMAPHORES += ["r%d_%d" % (_s, _w) for _w in range(MAXW)] + ["f%d_%d" % (_s, _w) for _w in range(MAXW)]


def _engines(mask):
    return [e for e in range(mask.bit_length()) if (mask >> e) & 1]


def _plan(cores, topo):
    def where(c):
        return (topo.host(c), topo.chip(c))

    rank = {c: i for i, c in enumerate(cores)}
    calls = {c: [] for c in cores}
    units = {c: [] for c in cores}
    passon = {c: {} for c in cores}
    sets, cfgs, peers_of = {}, {}, {}
    for c in cores:
        home = [d for d in cores if where(d) == where(c)]
        far = [d for d in cores if where(d) != where(c)]
        i = home.index(c)
        peers = home[i + 1:] + home[:i]
        off = _engines(topo.mask(c, far[0]))
        every = _engines(topo.mask(c, peers[0]))
        es = {"off": off, "all": every, "rest": [e for e in every if e not in off]}
        cfg = CFG["wide" if len(home) >= len(far) else "narrow"]
        sets[c], cfgs[c], peers_of[c] = es, cfg, peers
        q, base = rank[c], rank[c] * W
        whole = [("ld", 16)] + ([("ld2", 16)] if cfg["cut"] < W else [])
        if len(far) <= len(home):
            relays = [far[i * len(far) // len(home)]]
        else:
            k = len(far) // len(home)
            relays = far[i * k:(i + 1) * k]
        at = 0
        for w, cw in enumerate(cfg["waves"]):
            if i in cfg["hand"] and w == len(cfg["waves"]) - 1:
                k = cfg["hand"].index(i)
                hc = [d for d in range(SIM_CORES) if where(d) == where(c) and topo.die(d) != topo.die(c) and d not in rank][k]
                e, eh = es[cfg["hand_e"]], _engines(topo.mask(hc, far[0]))
                g0, g1 = base + at, base + at + cw
                calls[c].append((whole, [(g0, g1, [hc], e, "h")]))
                calls[hc] = [([("h", len(e))], [(g0, g1, far[k % len(far):] + far[:k % len(far)], eh, "v%d" % q)])]
                for d in far:
                    units[d].append((1.02 + 0.1 * w, "v%d" % q, len(eh), [(g0, g1)]))
                continue
            pw = cw // len(relays)
            e = es[cfg["relay_e"]]
            share = len(e) // len(relays)
            sem, trs = "r%d_%d" % (q, w), []
            for j, d in enumerate(relays):
                g0 = base + at + j * pw
                trs.append((g0, g0 + pw, [d], e[j * share:(j + 1) * share], sem))
                units[d].append((1 + 0.1 * w, sem, share, [(g0, g0 + pw)]))
                passon[d].setdefault(w, []).append((sem, share, g0, g0 + pw))
            at += cw
            calls[c].append((whole[:1] if at <= cfg["cut"] else whole, trs))
        e = es[cfg["near_e"]]
        calls[c].append((whole, [(base, base + W, peers, e, "n%d" % q)]))
        for d in peers:
            units[d].append((0, "n%d" % q, len(e), [(base, base + W)]))
    for c in cores:
        for w in sorted(passon[c]):
            got = sorted(passon[c][w], key=lambda p: p[2])
            runs = []
            for _sem, _n, g0, g1 in got:
                if runs and runs[-1][1] == g0:
                    runs[-1][1] = g1
                else:
                    runs.append([g0, g1])
            e = sets[c][cfgs[c]["fwd_e"]]
            share = len(e) // len(runs)
            sem = "f%d_%d" % (rank[c], w)
            trs = [(g0, g1, peers_of[c], e[j * share:(j + 1) * share], sem) for j, (g0, g1) in enumerate(runs)]
            calls[c].append(([(p[0], p[1]) for p in got], trs))
            for d in peers_of[c]:
                units[d].append((1.05 + 0.1 * w if len(passon[c]) > 1 else 3, sem, share * len(runs), [(g0, g1) for g0, g1 in runs]))
    return calls, units, cfgs


def _remote(g, core, T, topo, mine):
    X, sem, left = T.xs, T.sem, 0
    for waits, transfers in mine:
        for s, n in waits:
            g.wait_ge(sem[s], n)
        tl = []
        for g0, g1, dsts, engs, s in transfers:
            ids = []
            for d in dsts:
                rid, pid = topo.addr(d, core)
                ids.append(DstId(rid=rid, pnc=pid))
            mask = 0
            for e in engs:
                mask |= 1 << e
            tl.append(RemoteDMATransfer(dst_ids=ids, dma_engine_mask=mask, remote_sem=sem[s],
                                        srcs=[X[:, g0:g1]], dsts=[X[:, g0:g1] for _d in dsts]))
            left += len(engs)
        g.remote_dma_fused(tl, local_sem=sem.sent)
    g.wait_ge(sem.sent, left)


def rank_program(g, core, T, topo):
    r = T.rank_of(core)
    calls, units, cfgs = _plan(list(T.cores), topo)
    if r is None:
        if core in calls:
            _remote(g, core, T, topo, calls[core])
        return
    X, sem, cut = T.xs, T.sem, cfgs[core]["cut"]

    g.sync.dma_start(X[:, r * W:r * W + cut], T.x[:, 0:cut]).then_inc(sem.ld, 16)
    if cut < W:
        g.scalar.dma_start(X[:, r * W + cut:(r + 1) * W], T.x[:, cut:W]).then_inc(sem.ld2, 16)

    _remote(g, core, T, topo, calls[core])

    g.tensor.wait_ge(sem.ld, 16)
    if cut < W:
        g.tensor.wait_ge(sem.ld2, 16)
    have = {s: 0 for s in range(N)}
    ended = []
    todo = sorted(units[core], key=lambda u: (u[0], u[1]))
    for k, (when, s_name, n, ranges) in enumerate(todo):
        g.tensor.wait_ge(sem[s_name], n)
        for g0, g1 in ranges:
            for col in range(g0, g1, C):
                s, t = col // W, (col % W) // C
                mm = g.tensor.matmul(T["ps%d" % s][:, 0:C], X[:, r * W + t * C:r * W + (t + 1) * C], X[:, col:col + C],
                                     start=(have[s] == 0), stop=(have[s] == KT - 1))
                have[s] += 1
                if have[s] == KT:
                    mm.then_inc(sem["m%d" % s], 1)
                    ended.append((s, 0 if when < 1 else (3 if k == len(todo) - 1 or when >= 3 else 1)))

    for s, stage in ended:
        g.vector.wait_ge(sem["m%d" % s], 1)
        g.vector.tensor_copy(T.yb[:, s * C:(s + 1) * C], T["ps%d" % s][:, 0:C]).then_inc(sem["c%d" % stage], 1)

    stages = sorted({stage for _s2, stage in ended})
    count = {"sa": 0, "sb": 0}
    for stage in stages:
        q, qs = (g.sync, "sa") if stage == stages[-1] else (g.scalar, "sb")
        blocks = sorted(s for s, st in ended if st == stage)
        q.wait_ge(sem["c%d" % stage], len(blocks))
        b0 = prev = blocks[0]
        for b in blocks[1:] + [None]:
            if b is not None and b == prev + 1:
                prev = b
                continue
            q.dma_start(T.y[:, b0 * C:(prev + 1) * C], T.yb[:, b0 * C:(prev + 1) * C]).then_inc(sem[qs], 16)
            count[qs] += 16
            b0 = prev = b
    if count["sa"]:
        g.sync.wait_ge(sem.sa, count["sa"])
    if count["sb"]:
        g.scalar.wait_ge(sem.sb, count["sb"])
